import numpy as np
import ml_dtypes

BF16 = ml_dtypes.bfloat16


def bf(x):
    return np.asarray(x, np.float32).astype(BF16)


def f32(x):
    return np.asarray(x, np.float32)


def f64(x):
    return np.asarray(x).astype(np.float64)


def striped(idx):
    return np.tile(idx.reshape(-1, 16).T, (8, 1))


S, K, M, N = 512, 128, 256, 192


def setup_inputs():
    return {"base": bf(np.random.standard_normal((M, S))), "x": bf(np.random.standard_normal((K, N))), "w": bf(np.random.standard_normal((K, M)) / np.sqrt(K)), "b": f32(0.5 * np.random.standard_normal((M, 1))), "offs": striped(np.random.permutation(S)[:N])}


def reference(base, x, w, b, offs):
    idx = offs[:16].T.reshape(-1)
    z = f64(base).copy()
    z[:, idx] += f64(w).T @ f64(x)
    return np.maximum(z + f64(b), 0.0)

@@ -1,0 +1,54 @@
+import concourse.mybir as mybir
+from concourse.masks import make_identity
+
+P = 128
+M, S, K, N = 256, 512, 128, 192
+BLOCKS = M // P
+FLOPS = 2 * K * M * N
+
+BF16, F32, U16 = mybir.dt.bfloat16, mybir.dt.float32, mybir.dt.uint16
+ADD, MAX = mybir.AluOpType.add, mybir.AluOpType.max
+RELU = mybir.ActivationFunctionType.Relu
+
+
+def tile_scatter_matmul_kernel(tc, base, x, w, b, offs, out):
+    nc = tc.nc
+    with (
+        tc.tile_pool(name="held", bufs=1) as held,
+        tc.psum_pool(name="banks", bufs=1) as banks,
+    ):
+        offsets = held.tile([P, N // 16], U16, name="offsets")
+        nc.sync.dma_start(offsets[:], offs)
+        base_tiles = [held.tile([P, S], BF16, name=f"base{a}") for a in range(BLOCKS)]
+        nc.sync.dma_start(base_tiles[0][:], base[0:P, :])
+        nc.scalar.dma_start(base_tiles[1][:], base[P : 2 * P, :])
+        x_tile = held.tile([K, N], BF16, name="x_tile")
+        nc.sync.dma_start(x_tile[:], x)
+        w_tile = held.tile([K, M], BF16, name="w_tile")
+        nc.scalar.dma_start(w_tile[:], w)
+        bias = held.tile([P, BLOCKS], F32, name="bias")
+        with nc.allow_non_contiguous_dma(reason="one float32 of b to a partition"):
+            nc.scalar.dma_start(bias[:], b.rearrange("(a p) o -> p (a o)", p=P))
+
+        ident = held.tile([P, P], BF16, name="ident")
+        make_identity(nc, ident[:])
+
+        windows = [banks.tile([P, S], F32, name=f"window{a}") for a in range(BLOCKS)]
+        for a in range(BLOCKS):
+            nc.tensor.matmul(windows[a][:], ident[:], base_tiles[a][:], start=True, stop=False)
+
+        for a in range(BLOCKS):
+            nc.tensor.matmul(
+                windows[a][:].indirect(offsets[:]),
+                w_tile[:, a * P : (a + 1) * P],
+                x_tile[:],
+                start=False,
+                stop=True,
+            )
+
+        result0 = held.tile([P, S], F32, name="result0")
+        nc.scalar.activation(result0[:], windows[0][:], RELU, bias=bias[:, 0:1])
+        nc.sync.dma_start(out[0:P, :], result0[:])
+        result1 = held.tile([P, S], F32, name="result1")
+        nc.vector.tensor_scalar(result1[:], windows[1][:], bias[:, 1:2], 0.0, op0=ADD, op1=MAX)
+        nc.scalar.dma_start(out[P : 2 * P, :], result1[:])

@@ -20,8 +20,8 @@ def tile_scatter_matmul_kernel(tc, base, x, w, b, offs, out):
         offsets = held.tile([P, N // 16], U16, name="offsets")
         nc.sync.dma_start(offsets[:], offs)
         base_tiles = [held.tile([P, S], BF16, name=f"base{a}") for a in range(BLOCKS)]
-        nc.sync.dma_start(base_tiles[0][:], base[0:P, :])
-        nc.scalar.dma_start(base_tiles[1][:], base[P : 2 * P, :])
+        nc.scalar.dma_start(base_tiles[0][:], base[0:P, :])
+        nc.sync.dma_start(base_tiles[1][:], base[P : 2 * P, :])
         x_tile = held.tile([K, N], BF16, name="x_tile")
         nc.sync.dma_start(x_tile[:], x)
         w_tile = held.tile([K, M], BF16, name="w_tile")
@@ -32,6 +32,9 @@ def tile_scatter_matmul_kernel(tc, base, x, w, b, offs, out):
 
         ident = held.tile([P, P], BF16, name="ident")
         make_identity(nc, ident[:])
+
+        unread_relu = held.tile([P, 1], F32, name="unread_relu")
+        nc.scalar.activation(unread_relu[:], ident[:, 0:1], RELU)
 
         windows = [banks.tile([P, S], F32, name=f"window{a}") for a in range(BLOCKS)]
         for a in range(BLOCKS):

@@ -5,6 +5,7 @@ P = 128
 M, S, K, N = 256, 512, 128, 192
 BLOCKS = M // P
 FLOPS = 2 * K * M * N
+WARM_UPS = 12
 
 BF16, F32, U16 = mybir.dt.bfloat16, mybir.dt.float32, mybir.dt.uint16
 ADD, MAX = mybir.AluOpType.add, mybir.AluOpType.max
@@ -32,6 +33,12 @@ def tile_scatter_matmul_kernel(tc, base, x, w, b, offs, out):
 
         ident = held.tile([P, P], BF16, name="ident")
         make_identity(nc, ident[:])
+
+        zeros = held.tile([P, P], BF16, name="zeros")
+        nc.vector.memset(zeros[:], 0.0)
+        unread_bank = banks.tile([P, P], F32, name="unread_bank")
+        for i in range(WARM_UPS):
+            nc.tensor.matmul(unread_bank[:], zeros[:], zeros[:], start=True, stop=True)
 
         unread_relu = held.tile([P, 1], F32, name="unread_relu")
         nc.scalar.activation(unread_relu[:], ident[:, 0:1], RELU)

@@ -5,7 +5,7 @@ P = 128
 M, S, K, N = 256, 512, 128, 192
 BLOCKS = M // P
 FLOPS = 2 * K * M * N
-WARM_UPS = 12
+WARM_UPS = 3
 
 BF16, F32, U16 = mybir.dt.bfloat16, mybir.dt.float32, mybir.dt.uint16
 ADD, MAX = mybir.AluOpType.add, mybir.AluOpType.max
@@ -34,11 +34,17 @@ def tile_scatter_matmul_kernel(tc, base, x, w, b, offs, out):
         ident = held.tile([P, P], BF16, name="ident")
         make_identity(nc, ident[:])
 
-        zeros = held.tile([P, P], BF16, name="zeros")
-        nc.vector.memset(zeros[:], 0.0)
-        unread_bank = banks.tile([P, P], F32, name="unread_bank")
+        zero_pair = held.tile([P, 2], BF16, name="zero_pair")
+        nc.vector.memset(zero_pair[:], 0.0)
+        unread_bank = banks.tile([P, S], F32, name="unread_bank")
         for i in range(WARM_UPS):
-            nc.tensor.matmul(unread_bank[:], zeros[:], zeros[:], start=True, stop=True)
+            nc.tensor.matmul(
+                unread_bank[:],
+                zero_pair[:, 0:1].to_broadcast([P, P]),
+                zero_pair[:, 0:1].to_broadcast([P, S]),
+                start=True,
+                stop=True,
+            )
 
         unread_relu = held.tile([P, 1], F32, name="unread_relu")
         nc.scalar.activation(unread_relu[:], ident[:, 0:1], RELU)

@@ -63,8 +63,8 @@ def tile_scatter_matmul_kernel(tc, base, x, w, b, offs, out):
             )
 
         result0 = held.tile([P, S], F32, name="result0")
-        nc.scalar.activation(result0[:], windows[0][:], RELU, bias=bias[:, 0:1])
+        nc.vector.tensor_scalar(result0[:], windows[0][:], bias[:, 0:1], 0.0, op0=ADD, op1=MAX)
         nc.sync.dma_start(out[0:P, :], result0[:])
         result1 = held.tile([P, S], F32, name="result1")
-        nc.vector.tensor_scalar(result1[:], windows[1][:], bias[:, 1:2], 0.0, op0=ADD, op1=MAX)
+        nc.scalar.activation(result1[:], windows[1][:], RELU, bias=bias[:, 1:2])
         nc.scalar.dma_start(out[P : 2 * P, :], result1[:])

@@ -18,13 +18,13 @@ def tile_scatter_matmul_kernel(tc, base, x, w, b, offs, out):
         tc.tile_pool(name="held", bufs=1) as held,
         tc.psum_pool(name="banks", bufs=1) as banks,
     ):
+        base_tiles = [held.tile([P, S], BF16, name=f"base{a}") for a in range(BLOCKS)]
+        for a in range(BLOCKS):
+            nc.sync.dma_start(base_tiles[a][:], base[a * P : (a + 1) * P, :])
         offsets = held.tile([P, N // 16], U16, name="offsets")
         nc.sync.dma_start(offsets[:], offs)
-        base_tiles = [held.tile([P, S], BF16, name=f"base{a}") for a in range(BLOCKS)]
-        nc.scalar.dma_start(base_tiles[0][:], base[0:P, :])
-        nc.sync.dma_start(base_tiles[1][:], base[P : 2 * P, :])
         x_tile = held.tile([K, N], BF16, name="x_tile")
-        nc.sync.dma_start(x_tile[:], x)
+        nc.scalar.dma_start(x_tile[:], x)
         w_tile = held.tile([K, M], BF16, name="w_tile")
         nc.scalar.dma_start(w_tile[:], w)
         bias = held.tile([P, BLOCKS], F32, name="bias")

@@ -47,7 +47,7 @@ def tile_scatter_matmul_kernel(tc, base, x, w, b, offs, out):
             )
 
         unread_relu = held.tile([P, 1], F32, name="unread_relu")
-        nc.scalar.activation(unread_relu[:], ident[:, 0:1], RELU)
+        nc.scalar.activation(unread_relu[:], zero_pair[:, 0:1], RELU)
 
         windows = [banks.tile([P, S], F32, name=f"window{a}") for a in range(BLOCKS)]
         for a in range(BLOCKS):

@@ -19,14 +19,14 @@ def tile_scatter_matmul_kernel(tc, base, x, w, b, offs, out):
         tc.psum_pool(name="banks", bufs=1) as banks,
     ):
         base_tiles = [held.tile([P, S], BF16, name=f"base{a}") for a in range(BLOCKS)]
-        for a in range(BLOCKS):
-            nc.sync.dma_start(base_tiles[a][:], base[a * P : (a + 1) * P, :])
-        offsets = held.tile([P, N // 16], U16, name="offsets")
-        nc.sync.dma_start(offsets[:], offs)
+        nc.sync.dma_start(base_tiles[0][:], base[0:P, :])
+        nc.scalar.dma_start(base_tiles[1][:], base[P : 2 * P, :])
         x_tile = held.tile([K, N], BF16, name="x_tile")
-        nc.scalar.dma_start(x_tile[:], x)
+        nc.sync.dma_start(x_tile[:], x)
         w_tile = held.tile([K, M], BF16, name="w_tile")
         nc.scalar.dma_start(w_tile[:], w)
+        offsets = held.tile([P, N // 16], U16, name="offsets")
+        nc.sync.dma_start(offsets[:], offs)
         bias = held.tile([P, BLOCKS], F32, name="bias")
         with nc.allow_non_contiguous_dma(reason="one float32 of b to a partition"):
             nc.scalar.dma_start(bias[:], b.rearrange("(a p) o -> p (a o)", p=P))

import concourse.mybir as mybir
from concourse.masks import make_identity

P = 128
M, S, K, N = 256, 512, 128, 192
BLOCKS = M // P
FLOPS = 2 * K * M * N
WARM_UPS = 3

BF16, F32, U16 = mybir.dt.bfloat16, mybir.dt.float32, mybir.dt.uint16
ADD, MAX = mybir.AluOpType.add, mybir.AluOpType.max
RELU = mybir.ActivationFunctionType.Relu


def tile_scatter_matmul_kernel(tc, base, x, w, b, offs, out):
    nc = tc.nc
    with (
        tc.tile_pool(name="held", bufs=1) as held,
        tc.psum_pool(name="banks", bufs=1) as banks,
    ):
        base_tiles = [held.tile([P, S], BF16, name=f"base{a}") for a in range(BLOCKS)]
        nc.sync.dma_start(base_tiles[0][:], base[0:P, :])
        nc.scalar.dma_start(base_tiles[1][:], base[P : 2 * P, :])
        x_tile = held.tile([K, N], BF16, name="x_tile")
        nc.sync.dma_start(x_tile[:], x)
        w_tile = held.tile([K, M], BF16, name="w_tile")
        nc.scalar.dma_start(w_tile[:], w)
        offsets = held.tile([P, N // 16], U16, name="offsets")
        nc.sync.dma_start(offsets[:], offs)
        bias = held.tile([P, BLOCKS], F32, name="bias")
        with nc.allow_non_contiguous_dma(reason="one float32 of b to a partition"):
            nc.scalar.dma_start(bias[:], b.rearrange("(a p) o -> p (a o)", p=P))

        ident = held.tile([P, P], BF16, name="ident")
        make_identity(nc, ident[:])

        zero_pair = held.tile([P, 2], BF16, name="zero_pair")
        nc.vector.memset(zero_pair[:], 0.0)
        unread_bank = banks.tile([P, S], F32, name="unread_bank")
        for i in range(WARM_UPS):
            nc.tensor.matmul(
                unread_bank[:],
                zero_pair[:, 0:1].to_broadcast([P, P]),
                zero_pair[:, 0:1].to_broadcast([P, S]),
                start=True,
                stop=True,
            )

        unread_relu = held.tile([P, 1], F32, name="unread_relu")
        nc.scalar.activation(unread_relu[:], zero_pair[:, 0:1], RELU)

        windows = [banks.tile([P, S], F32, name=f"window{a}") for a in range(BLOCKS)]
        for a in range(BLOCKS):
            nc.tensor.matmul(windows[a][:], ident[:], base_tiles[a][:], start=True, stop=False)

        for a in range(BLOCKS):
            nc.tensor.matmul(
                windows[a][:].indirect(offsets[:]),
                w_tile[:, a * P : (a + 1) * P],
                x_tile[:],
                start=False,
                stop=True,
            )

        result0 = held.tile([P, S], F32, name="result0")
        nc.vector.tensor_scalar(result0[:], windows[0][:], bias[:, 0:1], 0.0, op0=ADD, op1=MAX)
        nc.sync.dma_start(out[0:P, :], result0[:])
        result1 = held.tile([P, S], F32, name="result1")
        nc.scalar.activation(result1[:], windows[1][:], RELU, bias=bias[:, 1:2])
        nc.scalar.dma_start(out[P : 2 * P, :], result1[:])
